import numpy as np
import ml_dtypes


def mxq(x, axis, fmt="e4m3"):
    dtype, down = {"e4m3": (ml_dtypes.float8_e4m3fn, 7), "e5m2": (ml_dtypes.float8_e5m2, 14)}[fmt]
    v = np.moveaxis(np.asarray(x, np.float32).astype(ml_dtypes.bfloat16).astype(np.float64), axis, -1)
    blocks = v.reshape(v.shape[:-1] + (-1, 32))
    amax = np.abs(blocks).max(-1, keepdims=True)
    byte = np.maximum(np.where(amax > 0, np.frexp(amax)[1] - 1 + 127, 0) - down, 1)
    scale = np.exp2(byte - 127.0)
    codes = (blocks / scale).astype(np.float32).astype(dtype).astype(np.float64)
    return np.moveaxis((codes * scale).reshape(v.shape), -1, axis)


WIDE = False


def mx_kscale(k):
    if not WIDE:
        return np.ones(k)
    levels = np.array([10, -10, 5, -5, 0])
    if k % 512:
        return np.exp2(np.random.permutation(np.resize(levels, k // 32))).repeat(32)
    a = np.empty((k // 512, 16))
    for p in range(k // 512):
        a[p, :8] = np.random.permutation(np.resize(levels, 8))
        for g in range(8):
            far = levels[np.abs(levels - a[p, g]) >= 10]
            a[p, g + 8] = far[np.random.randint(len(far))]
    return np.exp2(a.ravel()).repeat(32)


def f64(x):
    return np.asarray(x).astype(np.float64)


def striped8(idx):
    return np.asarray(idx).reshape(8, -1, 16).transpose(0, 2, 1).reshape(128, -1).astype(np.uint16)


def unstriped8(offs):
    return offs.reshape(8, 16, -1).transpose(0, 2, 1).reshape(8, -1).astype(np.int64)


def pick8(x, idx, run):
    r = np.arange(len(x))
    return x[r[:, None], idx[r % (8 * run) // run]]


E2M1 = np.array([0.0, 0.5, 1.0, 1.5, 2.0, 3.0, 4.0, 6.0, -0.0, -0.5, -1.0, -1.5, -2.0, -3.0, -4.0, -6.0])


def pack_weight(w, fmt):
    k, n = w.shape
    w = f64(np.asarray(w, np.float32).astype(ml_dtypes.bfloat16)).reshape(k // 32, 32, n)
    amax = np.abs(w).max(1)
    if fmt == "e4m3":
        byte = np.frexp(amax)[1] - 1 + 127 - 7
    else:
        mant, ex = np.frexp(amax / 6.0)
        byte = np.where(mant > 0.5, ex, ex - 1) + 127
    byte = np.clip(np.where(amax > 0, byte, 1), 1, 254)
    scaled = (w * np.exp2(127.0 - byte)[:, None, :]).reshape(k, n).astype(np.float32)
    by_word = np.ascontiguousarray(scaled.reshape(k // 512, 128, 4, n).transpose(0, 1, 3, 2))
    if fmt == "e4m3":
        words = by_word.astype(ml_dtypes.float8_e4m3fn).view(np.uint8)
    else:
        c = by_word.astype(ml_dtypes.float4_e2m1fn).view(np.uint8) & 0xF
        words = (c[..., 0::2] | (c[..., 1::2] << 4)).reshape(k // 512, 128, 2 * n)
    return np.ascontiguousarray(words), np.ascontiguousarray(byte.astype(np.uint8).reshape(k // 512, 16, n))


def unpack_weight(words, scales, fmt):
    g, _, n = scales.shape
    words = np.ascontiguousarray(words).reshape(g, 128, n, -1)
    if fmt == "e4m3":
        vals = words.view(ml_dtypes.float8_e4m3fn).astype(np.float64)
    else:
        nib = np.empty((g, 128, n, 4), np.uint8)
        nib[..., 0::2] = words & 0xF
        nib[..., 1::2] = words >> 4
        vals = E2M1[nib]
    vals = vals * np.repeat(np.exp2(scales.astype(np.float64) - 127.0), 8, axis=1)[..., None]
    return vals.transpose(0, 1, 3, 2).reshape(g * 512, n)


D, K, T, U, X, I, Q = 512, 512, 1024, 1024, 1024, 512, 128


def setup_inputs():
    n = np.random.standard_normal
    idx = np.stack([np.random.permutation(T)[:I] for _ in range(8)])
    idx2 = np.stack([np.random.permutation(U)[:I] for _ in range(8)])
    idx3 = np.stack([np.random.permutation(X)[:I] for _ in range(8)])
    idx4 = np.stack([np.random.permutation(X)[:I] for _ in range(8)])
    fd = mx_kscale(D)
    fk = mx_kscale(K)
    wqp = pack_weight(n((D, K)) * 1.0 / np.sqrt(D) * fd[:, None] * fk, "e4m3")
    cachep = pack_weight(n((K, T)) * 1.0 / np.sqrt(K) / fk[:, None], "e4m3")
    draftp = pack_weight(n((K, U)) * 1.0 / np.sqrt(K) / fk[:, None], "e2m1")
    archp = pack_weight(n((D, X)) * 1.0 / np.sqrt(D) * fd[:, None], "e4m3")
    return {
        "states": (n((D, Q)) * 0.95 / fd[:, None]).astype(np.float32),
        "wq_words": wqp[0],
        "wq_scales": wqp[1],
        "cache_words": cachep[0],
        "cache_scales": cachep[1],
        "draft_words": draftp[0],
        "draft_scales": draftp[1],
        "arch_words": archp[0],
        "arch_scales": archp[1],
        "offs": striped8(idx),
        "offs2": striped8(idx2),
        "offs3": striped8(idx3),
        "offs4": striped8(idx4),
    }


def reference(states, wq_words, wq_scales, cache_words, cache_scales, draft_words, draft_scales, arch_words, arch_scales, offs, offs2, offs3, offs4):
    idx = unstriped8(offs)
    idx2 = unstriped8(offs2)
    idx3 = unstriped8(offs3)
    idx4 = unstriped8(offs4)
    wqu = unpack_weight(wq_words, wq_scales, "e4m3")
    cacheu = unpack_weight(cache_words, cache_scales, "e4m3")
    draftu = unpack_weight(draft_words, draft_scales, "e2m1")
    archu = unpack_weight(arch_words, arch_scales, "e4m3")
    statesq = mxq(f64(states), 0, "e4m3")
    qv = wqu.T @ statesq
    qvq = mxq(qv, 0, "e4m3")
    a = qvq.T @ cacheu
    b = qvq.T @ draftu
    c0 = statesq.T @ archu
    w = np.abs(pick8(a, idx, 16) - pick8(b, idx2, 16))
    v = np.abs(pick8(b, idx2, 16) - pick8(c0, idx3, 16))
    r = w - v
    f1 = np.zeros((Q, X))
    f1[np.arange(Q)[:, None], idx4[np.arange(Q) % 128 // 16]] = r
    cc = c0 + f1
    y = np.abs(pick8(cc, idx3, 16) - w)
    return y

@@ -1,0 +1,187 @@
+from contextlib import ExitStack
+
+import concourse.mybir as mybir
+
+FLOPS = 469762048
+
+F32 = mybir.dt.float32
+BF16 = mybir.dt.bfloat16
+I32 = mybir.dt.int32
+U32 = mybir.dt.uint32
+U16 = mybir.dt.uint16
+U8 = mybir.dt.uint8
+FP8X4 = mybir.dt.float8_e4m3fn_x4
+FP4X4 = mybir.dt.float4_e2m1fn_x4
+ALU = mybir.AluOpType
+ACT = mybir.ActivationFunctionType
+
+P = 128
+K = 512
+T = 1024
+SLOTS = 512
+HALF = 256
+BANK = 512
+
+
+def tile_attend_gapenergies_sidethree_kernel(tc, states, wq_words, wq_scales, cache_words, cache_scales,
+                                              draft_words, draft_scales, arch_words, arch_scales,
+                                              offs, offs2, offs3, offs4, out):
+    nc = tc.nc
+    with ExitStack() as ctx:
+        sb = ctx.enter_context(tc.tile_pool(name="sb", bufs=1))
+        ps = ctx.enter_context(tc.psum_pool(name="ps", bufs=1))
+
+        def sbuf(name, shape, dtype):
+            return sb.tile(shape, dtype, name=name, align_bytes=64)
+
+        list_a = sb.tile([P, SLOTS // 16], U16, name="list_a")
+        list_b = sb.tile([P, SLOTS // 16], U16, name="list_b")
+        list_c = sb.tile([P, SLOTS // 16], U16, name="list_c")
+        list_r = sb.tile([P, SLOTS // 16], U16, name="list_r")
+
+        planes = sbuf("planes", [P, 4 * T], U8)
+        wq_stage = sbuf("wq_stage", [4, 4 * K], U8)
+        wq_spread = sbuf("wq_spread", [P, K], U8)
+        wq_plane = sbuf("wq_plane", [P, K], U8)
+        st_raw = sbuf("st_raw", [P, 4, P], F32)
+        wq_raw = sbuf("wq_raw", [P, K], U32)
+        wq_dealt = sbuf("wq_dealt", [P, K], U32)
+        arch_w = sbuf("arch_w", [P, T], U32)
+        cache_w = sbuf("cache_w", [P, T], U32)
+        draft_w = sbuf("draft_w", [P, 2 * T], U8)
+        f1 = sbuf("f1", [P, T], F32)
+
+        planes_i = planes[:].bitcast(I32)
+        nc.vector.memset(planes_i[0:32, :], 0)
+        nc.vector.memset(wq_spread[:].bitcast(I32), 0)
+        nc.vector.memset(f1[:], 0.0)
+
+        def load_scale_rows(dst, scales):
+            nc.sync.dma_start(dst.rearrange("f (g n) -> f g n", g=4),
+                              scales[0].bitcast(I32).rearrange("(g f) n -> f g n", f=4))
+
+        def load_words(dst, words):
+            nc.sync.dma_start(dst[:].bitcast(I32), words[0].rearrange("p n t -> p (n t)").bitcast(I32))
+
+        load_scale_rows(wq_stage[:].bitcast(I32), wq_scales)
+        nc.sync.dma_start(st_raw[:], states.rearrange("(p j) q -> p j q", j=4))
+        load_words(wq_raw, wq_words)
+        load_scale_rows(planes_i[4:8, :], arch_scales)
+        load_scale_rows(planes_i[0:4, :], draft_scales)
+        load_scale_rows(planes_i[8:12, :], cache_scales)
+        load_words(arch_w, arch_words)
+        nc.sync.dma_start(draft_w[:].bitcast(I32), draft_words[0].bitcast(I32))
+        load_words(cache_w, cache_words)
+        nc.sync.dma_start(list_c[:], offs3)
+        nc.sync.dma_start(list_a[:], offs)
+        nc.sync.dma_start(list_r[:], offs4)
+        nc.sync.dma_start(list_b[:], offs2)
+
+        wq_stage_i = wq_stage[:].bitcast(I32)
+        wq_spread_i = wq_spread[:].bitcast(I32)
+        for g in range(4):
+            nc.vector.tensor_copy(wq_spread_i[32 * g:32 * g + 4, :], wq_stage_i[0:4, g * (K // 4):(g + 1) * (K // 4)])
+        nc.vector.tensor_copy(wq_plane[:].rearrange("p (t m) -> p t m", t=4),
+                              wq_spread[:].rearrange("p (m t) -> p t m", t=4))
+
+        st_bf = sbuf("st_bf", [P, P, 4], BF16)
+        nc.scalar.activation(st_bf[:].rearrange("p (c i) t -> p c t i", i=4),
+                             st_raw[:].rearrange("p t (c i) -> p c t i", i=4), ACT.Copy)
+        nc.vector.tensor_copy(wq_dealt[:].rearrange("p (t m) -> p m t", t=4),
+                       wq_raw[:].rearrange("p (m t) -> p m t", t=4))
+        st_codes = sbuf("st_codes", [P, P], U32)
+        st_plane = sbuf("st_plane", [P, P], U8)
+        nc.vector.quantize_mx(out=st_codes[:].bitcast(FP8X4), scales=st_plane[:],
+                              in_=st_bf[:].rearrange("p q t -> p (q t)"))
+
+        for g in range(1, 4):
+            nc.vector.tensor_copy(planes_i[32 * g:32 * g + 32, 0:T // 4], planes_i[0:32, g * (T // 4):(g + 1) * (T // 4)])
+
+        qv_ps = ps.tile([P, 4, P], F32, name="qv_ps")
+        for t in range(4):
+            nc.tensor.matmul_mx(out=qv_ps[:, t, :], lhsT=wq_dealt[:, t * P:(t + 1) * P].bitcast(FP8X4),
+                                lhsT_scale=wq_plane[:, t * P:(t + 1) * P],
+                                rhs=st_codes[:].bitcast(FP8X4), rhs_scale=st_plane[:], start=True, stop=True)
+
+        def scores(name, codes, plane, moving, row):
+            banks = []
+            for j in range(T // BANK):
+                bank = ps.tile([P, BANK], F32, name="%s_ps%d" % (name, j))
+                nc.tensor.matmul_mx(out=bank[:], lhsT=codes[:].bitcast(FP8X4), lhsT_scale=plane,
+                                    rhs=moving(j), rhs_scale=planes[row:P, j * BANK:(j + 1) * BANK],
+                                    start=True, stop=True)
+                banks.append(bank)
+            return banks
+
+        c0_ps = scores("c0", st_codes, st_plane[:], lambda j: arch_w[:, j * BANK:(j + 1) * BANK].bitcast(FP8X4), 4)
+
+        qv_bf = sbuf("qv_bf", [P, P, 4], BF16)
+        nc.scalar.copy(qv_bf[:], qv_ps[:].rearrange("p t q -> p q t"))
+        qv_codes = sbuf("qv_codes", [P, P], U32)
+        qv_plane = planes[:, 3 * T:3 * T + P]
+        nc.vector.quantize_mx(out=qv_codes[:].bitcast(FP8X4), scales=qv_plane,
+                              in_=qv_bf[:].rearrange("p q t -> p (q t)"))
+
+        c0 = sbuf("c0", [P, T], F32)
+        nc.scalar.copy(c0[:, 0:BANK], c0_ps[0][:])
+        nc.scalar.copy(c0[:, BANK:T], c0_ps[1][:])
+
+        b_ps = scores("b", qv_codes, qv_plane,
+                      lambda j: draft_w[:, 2 * j * BANK:2 * (j + 1) * BANK].bitcast(FP4X4), 0)
+        a_ps = scores("a", qv_codes, qv_plane, lambda j: cache_w[:, j * BANK:(j + 1) * BANK].bitcast(FP8X4), 8)
+
+        a = sbuf("a", [P, T], F32)
+        b = sbuf("b", [P, T], F32)
+        gb = sbuf("gb", [P, SLOTS], F32)
+        e = sbuf("e", [P, SLOTS], F32)
+        d1 = sbuf("d1", [P, HALF], F32)
+        v1 = sbuf("v1", [P, HALF], F32)
+        w = sbuf("w", [P, SLOTS], F32)
+        r = sbuf("r", [P, SLOTS], F32)
+
+        def look(window, lst, s):
+            return window[:].indirect(lst[:, s.start // 16:s.stop // 16])
+
+        def abs_v(dst, src):
+            nc.vector.scalar_tensor_tensor(dst, src, -1.0, src, ALU.mult, ALU.max)
+
+        h1, h2 = slice(0, HALF), slice(HALF, SLOTS)
+
+        q1, q2, q3, q4 = [slice(128 * i, 128 * (i + 1)) for i in range(4)]
+        nc.vector.tensor_copy(b[:, 0:BANK], b_ps[0][:])
+        nc.scalar.copy(b[:, BANK:T], b_ps[1][:])
+        nc.vector.tensor_copy(a[:, 0:BANK], a_ps[0][:])
+        nc.vector.tensor_copy(a[:, BANK:T], a_ps[1][:])
+        nc.scalar.activation(gb[:, h1], look(b, list_b, h1), ACT.Copy)
+        nc.scalar.activation(gb[:, h2], look(b, list_b, h2), ACT.Copy)
+        nc.vector.tensor_tensor(d1[:], look(a, list_a, h1), gb[:, h1], ALU.subtract)
+        nc.vector.tensor_tensor(e[:, h1], look(c0, list_c, h1), gb[:, h1], ALU.subtract)
+        nc.scalar.activation(w[:, h1], d1[:], ACT.Abs)
+        for q in (q1, q2):
+            nc.scalar.activation(v1[:, q], e[:, q], ACT.Abs)
+        nc.vector.tensor_tensor(e[:, h2], look(c0, list_c, h2), gb[:, h2], ALU.subtract)
+        for q in (q1, q2):
+            nc.vector.tensor_tensor(r[:, q], w[:, q], v1[:, q], ALU.subtract)
+            nc.scalar.activation(look(f1, list_r, q), r[:, q], ACT.Copy)
+        d2 = v1
+        v2 = e
+        nc.vector.tensor_tensor(d2[:], look(a, list_a, h2), gb[:, h2], ALU.subtract)
+        abs_v(v2[:, h1], e[:, h2])
+        for q, lo in ((q3, q1), (q4, q2)):
+            abs_v(w[:, q], d2[:, lo])
+        for q, lo in ((q3, q1), (q4, q2)):
+            nc.vector.tensor_tensor(r[:, q], w[:, q], v2[:, lo], ALU.subtract)
+            nc.scalar.activation(look(f1, list_r, q), r[:, q], ACT.Copy)
+
+        cc = sbuf("cc", [P, T], F32)
+        nc.vector.tensor_tensor(cc[:], c0[:], f1[:], ALU.add)
+        g2 = sbuf("g2", [P, HALF], F32)
+        z = sbuf("z", [P, SLOTS], F32)
+        y = sbuf("y", [P, SLOTS], F32)
+        nc.vector.tensor_tensor(z[:, h1], look(cc, list_c, h1), w[:, h1], ALU.subtract)
+        nc.scalar.activation(g2[:], look(cc, list_c, h2), ACT.Copy)
+        nc.scalar.activation(y[:, h1], z[:, h1], ACT.Abs)
+        nc.vector.tensor_tensor(z[:, h2], g2[:], w[:, h2], ALU.subtract)
+        nc.sync.dma_start(out[:, h1], y[:, h1])
+        nc.scalar.activation(y[:, h2], z[:, h2], ACT.Abs)
+        nc.sync.dma_start(out[:, h2], y[:, h2])

@@ -21,6 +21,7 @@ T = 1024
 SLOTS = 512
 HALF = 256
 BANK = 512
+CHUNK = 256
 
 
 def tile_attend_gapenergies_sidethree_kernel(tc, states, wq_words, wq_scales, cache_words, cache_scales,
@@ -39,22 +40,32 @@ def tile_attend_gapenergies_sidethree_kernel(tc, states, wq_words, wq_scales, ca
         list_c = sb.tile([P, SLOTS // 16], U16, name="list_c")
         list_r = sb.tile([P, SLOTS // 16], U16, name="list_r")
 
-        planes = sbuf("planes", [P, 4 * T], U8)
+        draft_plane = sbuf("draft_plane", [P, 4 * T], U8)
+        packed = sbuf("packed", [P, 2 * CHUNK], U8)
         wq_stage = sbuf("wq_stage", [4, 4 * K], U8)
         wq_spread = sbuf("wq_spread", [P, K], U8)
         wq_plane = sbuf("wq_plane", [P, K], U8)
         st_raw = sbuf("st_raw", [P, 4, P], F32)
         wq_raw = sbuf("wq_raw", [P, K], U32)
-        wq_dealt = sbuf("wq_dealt", [P, K], U32)
+        wq_dealt = [sbuf("wq_dealt%d" % u, [P, 2, P], U32) for u in range(2)]
         arch_w = sbuf("arch_w", [P, T], U32)
         cache_w = sbuf("cache_w", [P, T], U32)
         draft_w = sbuf("draft_w", [P, 2 * T], U8)
-        f1 = sbuf("f1", [P, T], F32)
+        f1 = [sbuf("f1_%d" % i, [P, T], F32) for i in range(2)]
 
-        planes_i = planes[:].bitcast(I32)
-        nc.vector.memset(planes_i[0:32, :], 0)
+        draft_i = draft_plane[:].bitcast(I32)
+        packed_i = packed[:].bitcast(I32)
+        nc.vector.memset(packed_i, 0)
         nc.vector.memset(wq_spread[:].bitcast(I32), 0)
-        nc.vector.memset(f1[:], 0.0)
+        nc.vector.memset(draft_i[:, 0:T // 4], 0)
+        for window in f1:
+            nc.vector.memset(window[:], 0.0)
+
+        def load_packed(col, scales):
+            rows = scales[0].bitcast(I32)
+            for g in range(4):
+                nc.sync.dma_start(packed_i[32 * g:32 * g + 16, col // 4:(col + CHUNK) // 4],
+                                  rows[4 * g:4 * g + 4, :].rearrange("f (j c) -> j f c", j=4))
 
         def load_scale_rows(dst, scales):
             nc.sync.dma_start(dst.rearrange("f (g n) -> f g n", g=4),
@@ -66,10 +77,10 @@ def tile_attend_gapenergies_sidethree_kernel(tc, states, wq_words, wq_scales, ca
         load_scale_rows(wq_stage[:].bitcast(I32), wq_scales)
         nc.sync.dma_start(st_raw[:], states.rearrange("(p j) q -> p j q", j=4))
         load_words(wq_raw, wq_words)
-        load_scale_rows(planes_i[4:8, :], arch_scales)
-        load_scale_rows(planes_i[0:4, :], draft_scales)
-        load_scale_rows(planes_i[8:12, :], cache_scales)
+        load_packed(0, arch_scales)
         load_words(arch_w, arch_words)
+        load_scale_rows(draft_i[0:4, :], draft_scales)
+        load_packed(CHUNK, cache_scales)
         nc.sync.dma_start(draft_w[:].bitcast(I32), draft_words[0].bitcast(I32))
         load_words(cache_w, cache_words)
         nc.sync.dma_start(list_c[:], offs3)
@@ -87,38 +98,39 @@ def tile_attend_gapenergies_sidethree_kernel(tc, states, wq_words, wq_scales, ca
         st_bf = sbuf("st_bf", [P, P, 4], BF16)
         nc.scalar.activation(st_bf[:].rearrange("p (c i) t -> p c t i", i=4),
                              st_raw[:].rearrange("p t (c i) -> p c t i", i=4), ACT.Copy)
-        nc.vector.tensor_copy(wq_dealt[:].rearrange("p (t m) -> p m t", t=4),
-                       wq_raw[:].rearrange("p (m t) -> p m t", t=4))
+        plain = wq_raw[:].rearrange("p (m t) -> p m t", t=4)
+        nc.vector.tensor_copy(wq_dealt[0][:].rearrange("p t m -> p m t"), plain[:, :, 0:2])
+        nc.scalar.copy(wq_dealt[1][:].rearrange("p t m -> p m t"), plain[:, :, 2:4])
         st_codes = sbuf("st_codes", [P, P], U32)
         st_plane = sbuf("st_plane", [P, P], U8)
         nc.vector.quantize_mx(out=st_codes[:].bitcast(FP8X4), scales=st_plane[:],
                               in_=st_bf[:].rearrange("p q t -> p (q t)"))
 
         for g in range(1, 4):
-            nc.vector.tensor_copy(planes_i[32 * g:32 * g + 32, 0:T // 4], planes_i[0:32, g * (T // 4):(g + 1) * (T // 4)])
+            nc.vector.tensor_copy(draft_i[32 * g:32 * g + 4, 0:T // 4], draft_i[0:4, g * (T // 4):(g + 1) * (T // 4)])
 
         qv_ps = ps.tile([P, 4, P], F32, name="qv_ps")
         for t in range(4):
-            nc.tensor.matmul_mx(out=qv_ps[:, t, :], lhsT=wq_dealt[:, t * P:(t + 1) * P].bitcast(FP8X4),
+            nc.tensor.matmul_mx(out=qv_ps[:, t, :], lhsT=wq_dealt[t // 2][:, t % 2, :].bitcast(FP8X4),
                                 lhsT_scale=wq_plane[:, t * P:(t + 1) * P],
                                 rhs=st_codes[:].bitcast(FP8X4), rhs_scale=st_plane[:], start=True, stop=True)
 
-        def scores(name, codes, plane, moving, row):
-            banks = []
-            for j in range(T // BANK):
-                bank = ps.tile([P, BANK], F32, name="%s_ps%d" % (name, j))
-                nc.tensor.matmul_mx(out=bank[:], lhsT=codes[:].bitcast(FP8X4), lhsT_scale=plane,
-                                    rhs=moving(j), rhs_scale=planes[row:P, j * BANK:(j + 1) * BANK],
-                                    start=True, stop=True)
-                banks.append(bank)
+        def scores(name, codes, plane, width, moving, moving_plane):
+            banks = [ps.tile([P, BANK], F32, name="%s_ps%d" % (name, i)) for i in range(T // BANK)]
+            for j in range(T // width):
+                lo = j * width % BANK
+                nc.tensor.matmul_mx(out=banks[j * width // BANK][:, lo:lo + width], lhsT=codes[:].bitcast(FP8X4),
+                                    lhsT_scale=plane, rhs=moving(j), rhs_scale=moving_plane(j), start=True, stop=True)
             return banks
 
-        c0_ps = scores("c0", st_codes, st_plane[:], lambda j: arch_w[:, j * BANK:(j + 1) * BANK].bitcast(FP8X4), 4)
+        c0_ps = scores("c0", st_codes, st_plane[:], CHUNK,
+                       lambda j: arch_w[:, j * CHUNK:(j + 1) * CHUNK].bitcast(FP8X4),
+                       lambda j: packed[4 * j:P, 0:CHUNK])
 
         qv_bf = sbuf("qv_bf", [P, P, 4], BF16)
         nc.scalar.copy(qv_bf[:], qv_ps[:].rearrange("p t q -> p q t"))
         qv_codes = sbuf("qv_codes", [P, P], U32)
-        qv_plane = planes[:, 3 * T:3 * T + P]
+        qv_plane = draft_plane[:, 3 * T:3 * T + P]
         nc.vector.quantize_mx(out=qv_codes[:].bitcast(FP8X4), scales=qv_plane,
                               in_=qv_bf[:].rearrange("p q t -> p (q t)"))
 
@@ -126,9 +138,12 @@ def tile_attend_gapenergies_sidethree_kernel(tc, states, wq_words, wq_scales, ca
         nc.scalar.copy(c0[:, 0:BANK], c0_ps[0][:])
         nc.scalar.copy(c0[:, BANK:T], c0_ps[1][:])
 
-        b_ps = scores("b", qv_codes, qv_plane,
-                      lambda j: draft_w[:, 2 * j * BANK:2 * (j + 1) * BANK].bitcast(FP4X4), 0)
-        a_ps = scores("a", qv_codes, qv_plane, lambda j: cache_w[:, j * BANK:(j + 1) * BANK].bitcast(FP8X4), 8)
+        b_ps = scores("b", qv_codes, qv_plane, BANK,
+                      lambda j: draft_w[:, 2 * j * BANK:2 * (j + 1) * BANK].bitcast(FP4X4),
+                      lambda j: draft_plane[:, j * BANK:(j + 1) * BANK])
+        a_ps = scores("a", qv_codes, qv_plane, CHUNK,
+                      lambda j: cache_w[:, j * CHUNK:(j + 1) * CHUNK].bitcast(FP8X4),
+                      lambda j: packed[4 * j:P, CHUNK:2 * CHUNK])
 
         a = sbuf("a", [P, T], F32)
         b = sbuf("b", [P, T], F32)
@@ -160,28 +175,31 @@ def tile_attend_gapenergies_sidethree_kernel(tc, states, wq_words, wq_scales, ca
         for q in (q1, q2):
             nc.scalar.activation(v1[:, q], e[:, q], ACT.Abs)
         nc.vector.tensor_tensor(e[:, h2], look(c0, list_c, h2), gb[:, h2], ALU.subtract)
-        for q in (q1, q2):
+        for q, window in zip((q1, q2), f1):
             nc.vector.tensor_tensor(r[:, q], w[:, q], v1[:, q], ALU.subtract)
-            nc.scalar.activation(look(f1, list_r, q), r[:, q], ACT.Copy)
+            nc.scalar.activation(look(window, list_r, q), r[:, q], ACT.Copy)
         d2 = v1
         v2 = e
         nc.vector.tensor_tensor(d2[:], look(a, list_a, h2), gb[:, h2], ALU.subtract)
         abs_v(v2[:, h1], e[:, h2])
-        for q, lo in ((q3, q1), (q4, q2)):
-            abs_v(w[:, q], d2[:, lo])
-        for q, lo in ((q3, q1), (q4, q2)):
+        abs_v(w[:, h2], d2[:])
+        for q, lo, window in zip((slice(256, 320), slice(320, 512)), (slice(0, 64), slice(64, 256)), f1):
             nc.vector.tensor_tensor(r[:, q], w[:, q], v2[:, lo], ALU.subtract)
-            nc.scalar.activation(look(f1, list_r, q), r[:, q], ACT.Copy)
+            nc.scalar.activation(look(window, list_r, q), r[:, q], ACT.Copy)
 
         cc = sbuf("cc", [P, T], F32)
-        nc.vector.tensor_tensor(cc[:], c0[:], f1[:], ALU.add)
+        part = sbuf("part", [P, T], F32)
+        nc.vector.tensor_tensor(part[:], c0[:], f1[0][:], ALU.add)
+        nc.vector.tensor_tensor(cc[:], part[:], f1[1][:], ALU.add)
         g2 = sbuf("g2", [P, HALF], F32)
         z = sbuf("z", [P, SLOTS], F32)
         y = sbuf("y", [P, SLOTS], F32)
         nc.vector.tensor_tensor(z[:, h1], look(cc, list_c, h1), w[:, h1], ALU.subtract)
         nc.scalar.activation(g2[:], look(cc, list_c, h2), ACT.Copy)
         nc.scalar.activation(y[:, h1], z[:, h1], ACT.Abs)
-        nc.vector.tensor_tensor(z[:, h2], g2[:], w[:, h2], ALU.subtract)
+        for q, lo in ((q3, q1), (q4, q2)):
+            nc.vector.tensor_tensor(z[:, q], g2[:, lo], w[:, q], ALU.subtract)
         nc.sync.dma_start(out[:, h1], y[:, h1])
-        nc.scalar.activation(y[:, h2], z[:, h2], ACT.Abs)
+        abs_v(y[:, q3], z[:, q3])
+        nc.scalar.activation(y[:, q4], z[:, q4], ACT.Abs)
         nc.sync.dma_start(out[:, h2], y[:, h2])

@@ -22,6 +22,7 @@ SLOTS = 512
 HALF = 256
 BANK = 512
 CHUNK = 256
+SPLIT = 768
 
 
 def tile_attend_gapenergies_sidethree_kernel(tc, states, wq_words, wq_scales, cache_words, cache_scales,
@@ -47,19 +48,18 @@ def tile_attend_gapenergies_sidethree_kernel(tc, states, wq_words, wq_scales, ca
         wq_plane = sbuf("wq_plane", [P, K], U8)
         st_raw = sbuf("st_raw", [P, 4, P], F32)
         wq_raw = sbuf("wq_raw", [P, K], U32)
-        wq_dealt = [sbuf("wq_dealt%d" % u, [P, 2, P], U32) for u in range(2)]
+        wq_dealt = sbuf("wq_dealt", [P, K], U32)
         arch_w = sbuf("arch_w", [P, T], U32)
         cache_w = sbuf("cache_w", [P, T], U32)
         draft_w = sbuf("draft_w", [P, 2 * T], U8)
-        f1 = [sbuf("f1_%d" % i, [P, T], F32) for i in range(2)]
+        f1 = sbuf("f1", [P, T], F32)
 
         draft_i = draft_plane[:].bitcast(I32)
         packed_i = packed[:].bitcast(I32)
         nc.vector.memset(packed_i, 0)
         nc.vector.memset(wq_spread[:].bitcast(I32), 0)
         nc.vector.memset(draft_i[:, 0:T // 4], 0)
-        for window in f1:
-            nc.vector.memset(window[:], 0.0)
+        nc.vector.memset(f1[:], 0.0)
 
         def load_packed(col, scales):
             rows = scales[0].bitcast(I32)
@@ -80,13 +80,13 @@ def tile_attend_gapenergies_sidethree_kernel(tc, states, wq_words, wq_scales, ca
         load_packed(0, arch_scales)
         load_words(arch_w, arch_words)
         load_scale_rows(draft_i[0:4, :], draft_scales)
-        load_packed(CHUNK, cache_scales)
         nc.sync.dma_start(draft_w[:].bitcast(I32), draft_words[0].bitcast(I32))
         load_words(cache_w, cache_words)
-        nc.sync.dma_start(list_c[:], offs3)
+        load_packed(CHUNK, cache_scales)
         nc.sync.dma_start(list_a[:], offs)
-        nc.sync.dma_start(list_r[:], offs4)
         nc.sync.dma_start(list_b[:], offs2)
+        nc.sync.dma_start(list_c[:], offs3)
+        nc.sync.dma_start(list_r[:], offs4)
 
         wq_stage_i = wq_stage[:].bitcast(I32)
         wq_spread_i = wq_spread[:].bitcast(I32)
@@ -98,9 +98,8 @@ def tile_attend_gapenergies_sidethree_kernel(tc, states, wq_words, wq_scales, ca
         st_bf = sbuf("st_bf", [P, P, 4], BF16)
         nc.scalar.activation(st_bf[:].rearrange("p (c i) t -> p c t i", i=4),
                              st_raw[:].rearrange("p t (c i) -> p c t i", i=4), ACT.Copy)
-        plain = wq_raw[:].rearrange("p (m t) -> p m t", t=4)
-        nc.vector.tensor_copy(wq_dealt[0][:].rearrange("p t m -> p m t"), plain[:, :, 0:2])
-        nc.scalar.copy(wq_dealt[1][:].rearrange("p t m -> p m t"), plain[:, :, 2:4])
+        nc.vector.tensor_copy(wq_dealt[:].rearrange("p (t m) -> p m t", t=4),
+                              wq_raw[:].rearrange("p (m t) -> p m t", t=4))
         st_codes = sbuf("st_codes", [P, P], U32)
         st_plane = sbuf("st_plane", [P, P], U8)
         nc.vector.quantize_mx(out=st_codes[:].bitcast(FP8X4), scales=st_plane[:],
@@ -111,7 +110,7 @@ def tile_attend_gapenergies_sidethree_kernel(tc, states, wq_words, wq_scales, ca
 
         qv_ps = ps.tile([P, 4, P], F32, name="qv_ps")
         for t in range(4):
-            nc.tensor.matmul_mx(out=qv_ps[:, t, :], lhsT=wq_dealt[t // 2][:, t % 2, :].bitcast(FP8X4),
+            nc.tensor.matmul_mx(out=qv_ps[:, t, :], lhsT=wq_dealt[:, t * P:(t + 1) * P].bitcast(FP8X4),
                                 lhsT_scale=wq_plane[:, t * P:(t + 1) * P],
                                 rhs=st_codes[:].bitcast(FP8X4), rhs_scale=st_plane[:], start=True, stop=True)
 
@@ -147,12 +146,18 @@ def tile_attend_gapenergies_sidethree_kernel(tc, states, wq_words, wq_scales, ca
 
         a = sbuf("a", [P, T], F32)
         b = sbuf("b", [P, T], F32)
-        gb = sbuf("gb", [P, SLOTS], F32)
-        e = sbuf("e", [P, SLOTS], F32)
+        gb1 = sbuf("gb1", [P, HALF], F32)
+        gc2 = sbuf("gc2", [P, HALF], F32)
         d1 = sbuf("d1", [P, HALF], F32)
-        v1 = sbuf("v1", [P, HALF], F32)
+        e1 = sbuf("e1", [P, HALF], F32)
+        v2 = sbuf("v2", [P, HALF], F32)
         w = sbuf("w", [P, SLOTS], F32)
         r = sbuf("r", [P, SLOTS], F32)
+        gc1_gb2 = sbuf("gc1_gb2", [P, 3 * 128], F32)
+        gc1, gb2 = gc1_gb2[:, 128:384], gc1_gb2[:, 0:256]
+        d2 = sbuf("d2", [P, HALF], F32)
+        e2 = sbuf("e2", [P, HALF], F32)
+        v1 = [d2[:, 0:128], e2[:, 0:128]]
 
         def look(window, lst, s):
             return window[:].indirect(lst[:, s.start // 16:s.stop // 16])
@@ -167,30 +172,30 @@ def tile_attend_gapenergies_sidethree_kernel(tc, states, wq_words, wq_scales, ca
         nc.scalar.copy(b[:, BANK:T], b_ps[1][:])
         nc.vector.tensor_copy(a[:, 0:BANK], a_ps[0][:])
         nc.vector.tensor_copy(a[:, BANK:T], a_ps[1][:])
-        nc.scalar.activation(gb[:, h1], look(b, list_b, h1), ACT.Copy)
-        nc.scalar.activation(gb[:, h2], look(b, list_b, h2), ACT.Copy)
-        nc.vector.tensor_tensor(d1[:], look(a, list_a, h1), gb[:, h1], ALU.subtract)
-        nc.vector.tensor_tensor(e[:, h1], look(c0, list_c, h1), gb[:, h1], ALU.subtract)
-        nc.scalar.activation(w[:, h1], d1[:], ACT.Abs)
+        nc.scalar.activation(gb1[:], look(b, list_b, h1), ACT.Copy)
+        nc.scalar.activation(gc1, look(c0, list_c, h1), ACT.Copy)
+        nc.scalar.activation(gc2[:], look(c0, list_c, h2), ACT.Copy)
+        nc.vector.tensor_tensor(d1[:], look(a, list_a, h1), gb1[:], ALU.subtract)
         for q in (q1, q2):
-            nc.scalar.activation(v1[:, q], e[:, q], ACT.Abs)
-        nc.vector.tensor_tensor(e[:, h2], look(c0, list_c, h2), gb[:, h2], ALU.subtract)
-        for q, window in zip((q1, q2), f1):
-            nc.vector.tensor_tensor(r[:, q], w[:, q], v1[:, q], ALU.subtract)
-            nc.scalar.activation(look(window, list_r, q), r[:, q], ACT.Copy)
-        d2 = v1
-        v2 = e
-        nc.vector.tensor_tensor(d2[:], look(a, list_a, h2), gb[:, h2], ALU.subtract)
-        abs_v(v2[:, h1], e[:, h2])
+            nc.vector.tensor_tensor(e1[:, q], gc1[:, q], gb1[:, q], ALU.subtract)
+        nc.vector.tensor_copy(gb2, look(b, list_b, h2))
+        for q, v in zip((q1, q2), v1):
+            nc.scalar.activation(w[:, q], d1[:, q], ACT.Abs)
+            nc.scalar.activation(v, e1[:, q], ACT.Abs)
+        for q, v in zip((q1, q2), v1):
+            nc.vector.tensor_tensor(r[:, q], w[:, q], v, ALU.subtract)
+        nc.scalar.activation(look(f1, list_r, h1), r[:, h1], ACT.Copy)
+        nc.vector.tensor_tensor(d2[:], look(a, list_a, h2), gb2, ALU.subtract)
+        nc.vector.tensor_tensor(e2[:], gc2[:], gb2, ALU.subtract)
         abs_v(w[:, h2], d2[:])
-        for q, lo, window in zip((slice(256, 320), slice(320, 512)), (slice(0, 64), slice(64, 256)), f1):
-            nc.vector.tensor_tensor(r[:, q], w[:, q], v2[:, lo], ALU.subtract)
-            nc.scalar.activation(look(window, list_r, q), r[:, q], ACT.Copy)
+        abs_v(v2[:], e2[:])
+        nc.vector.tensor_tensor(r[:, h2], w[:, h2], v2[:], ALU.subtract)
+        nc.scalar.activation(look(f1, list_r, h2), r[:, h2], ACT.Copy)
 
         cc = sbuf("cc", [P, T], F32)
-        part = sbuf("part", [P, T], F32)
-        nc.vector.tensor_tensor(part[:], c0[:], f1[0][:], ALU.add)
-        nc.vector.tensor_tensor(cc[:], part[:], f1[1][:], ALU.add)
+        nc.vector.tensor_tensor(cc[:, 0:BANK], c0_ps[0][:], f1[:, 0:BANK], ALU.add)
+        nc.vector.tensor_tensor(cc[:, BANK:SPLIT], c0_ps[1][:, 0:SPLIT - BANK], f1[:, BANK:SPLIT], ALU.add)
+        nc.gpsimd.tensor_tensor(cc[:, SPLIT:T], c0[:, SPLIT:T], f1[:, SPLIT:T], ALU.add)
         g2 = sbuf("g2", [P, HALF], F32)
         z = sbuf("z", [P, SLOTS], F32)
         y = sbuf("y", [P, SLOTS], F32)

from contextlib import ExitStack

import concourse.mybir as mybir

FLOPS = 469762048

F32 = mybir.dt.float32
BF16 = mybir.dt.bfloat16
I32 = mybir.dt.int32
U32 = mybir.dt.uint32
U16 = mybir.dt.uint16
U8 = mybir.dt.uint8
FP8X4 = mybir.dt.float8_e4m3fn_x4
FP4X4 = mybir.dt.float4_e2m1fn_x4
ALU = mybir.AluOpType
ACT = mybir.ActivationFunctionType

P = 128
K = 512
T = 1024
SLOTS = 512
HALF = 256
BANK = 512
CHUNK = 256
SPLIT = 768


def tile_attend_gapenergies_sidethree_kernel(tc, states, wq_words, wq_scales, cache_words, cache_scales,
                                              draft_words, draft_scales, arch_words, arch_scales,
                                              offs, offs2, offs3, offs4, out):
    nc = tc.nc
    with ExitStack() as ctx:
        sb = ctx.enter_context(tc.tile_pool(name="sb", bufs=1))
        ps = ctx.enter_context(tc.psum_pool(name="ps", bufs=1))

        def sbuf(name, shape, dtype):
            return sb.tile(shape, dtype, name=name, align_bytes=64)

        list_a = sb.tile([P, SLOTS // 16], U16, name="list_a")
        list_b = sb.tile([P, SLOTS // 16], U16, name="list_b")
        list_c = sb.tile([P, SLOTS // 16], U16, name="list_c")
        list_r = sb.tile([P, SLOTS // 16], U16, name="list_r")

        draft_plane = sbuf("draft_plane", [P, 4 * T], U8)
        packed = sbuf("packed", [P, 2 * CHUNK], U8)
        wq_stage = sbuf("wq_stage", [4, 4 * K], U8)
        wq_spread = sbuf("wq_spread", [P, K], U8)
        wq_plane = sbuf("wq_plane", [P, K], U8)
        st_raw = sbuf("st_raw", [P, 4, P], F32)
        wq_raw = sbuf("wq_raw", [P, K], U32)
        wq_dealt = sbuf("wq_dealt", [P, K], U32)
        arch_w = sbuf("arch_w", [P, T], U32)
        cache_w = sbuf("cache_w", [P, T], U32)
        draft_w = sbuf("draft_w", [P, 2 * T], U8)
        f1 = sbuf("f1", [P, T], F32)

        draft_i = draft_plane[:].bitcast(I32)
        packed_i = packed[:].bitcast(I32)
        nc.vector.memset(packed_i, 0)
        nc.vector.memset(wq_spread[:].bitcast(I32), 0)
        nc.vector.memset(draft_i[:, 0:T // 4], 0)
        nc.vector.memset(f1[:], 0.0)

        def load_packed(col, scales):
            rows = scales[0].bitcast(I32)
            for g in range(4):
                nc.sync.dma_start(packed_i[32 * g:32 * g + 16, col // 4:(col + CHUNK) // 4],
                                  rows[4 * g:4 * g + 4, :].rearrange("f (j c) -> j f c", j=4))

        def load_scale_rows(dst, scales):
            nc.sync.dma_start(dst.rearrange("f (g n) -> f g n", g=4),
                              scales[0].bitcast(I32).rearrange("(g f) n -> f g n", f=4))

        def load_words(dst, words):
            nc.sync.dma_start(dst[:].bitcast(I32), words[0].rearrange("p n t -> p (n t)").bitcast(I32))

        load_scale_rows(wq_stage[:].bitcast(I32), wq_scales)
        nc.sync.dma_start(st_raw[:], states.rearrange("(p j) q -> p j q", j=4))
        load_words(wq_raw, wq_words)
        load_packed(0, arch_scales)
        load_words(arch_w, arch_words)
        load_scale_rows(draft_i[0:4, :], draft_scales)
        nc.sync.dma_start(draft_w[:].bitcast(I32), draft_words[0].bitcast(I32))
        load_words(cache_w, cache_words)
        load_packed(CHUNK, cache_scales)
        nc.sync.dma_start(list_a[:], offs)
        nc.sync.dma_start(list_b[:], offs2)
        nc.sync.dma_start(list_c[:], offs3)
        nc.sync.dma_start(list_r[:], offs4)

        wq_stage_i = wq_stage[:].bitcast(I32)
        wq_spread_i = wq_spread[:].bitcast(I32)
        for g in range(4):
            nc.vector.tensor_copy(wq_spread_i[32 * g:32 * g + 4, :], wq_stage_i[0:4, g * (K // 4):(g + 1) * (K // 4)])
        nc.vector.tensor_copy(wq_plane[:].rearrange("p (t m) -> p t m", t=4),
                              wq_spread[:].rearrange("p (m t) -> p t m", t=4))

        st_bf = sbuf("st_bf", [P, P, 4], BF16)
        nc.scalar.activation(st_bf[:].rearrange("p (c i) t -> p c t i", i=4),
                             st_raw[:].rearrange("p t (c i) -> p c t i", i=4), ACT.Copy)
        nc.vector.tensor_copy(wq_dealt[:].rearrange("p (t m) -> p m t", t=4),
                              wq_raw[:].rearrange("p (m t) -> p m t", t=4))
        st_codes = sbuf("st_codes", [P, P], U32)
        st_plane = sbuf("st_plane", [P, P], U8)
        nc.vector.quantize_mx(out=st_codes[:].bitcast(FP8X4), scales=st_plane[:],
                              in_=st_bf[:].rearrange("p q t -> p (q t)"))

        for g in range(1, 4):
            nc.vector.tensor_copy(draft_i[32 * g:32 * g + 4, 0:T // 4], draft_i[0:4, g * (T // 4):(g + 1) * (T // 4)])

        qv_ps = ps.tile([P, 4, P], F32, name="qv_ps")
        for t in range(4):
            nc.tensor.matmul_mx(out=qv_ps[:, t, :], lhsT=wq_dealt[:, t * P:(t + 1) * P].bitcast(FP8X4),
                                lhsT_scale=wq_plane[:, t * P:(t + 1) * P],
                                rhs=st_codes[:].bitcast(FP8X4), rhs_scale=st_plane[:], start=True, stop=True)

        def scores(name, codes, plane, width, moving, moving_plane):
            banks = [ps.tile([P, BANK], F32, name="%s_ps%d" % (name, i)) for i in range(T // BANK)]
            for j in range(T // width):
                lo = j * width % BANK
                nc.tensor.matmul_mx(out=banks[j * width // BANK][:, lo:lo + width], lhsT=codes[:].bitcast(FP8X4),
                                    lhsT_scale=plane, rhs=moving(j), rhs_scale=moving_plane(j), start=True, stop=True)
            return banks

        c0_ps = scores("c0", st_codes, st_plane[:], CHUNK,
                       lambda j: arch_w[:, j * CHUNK:(j + 1) * CHUNK].bitcast(FP8X4),
                       lambda j: packed[4 * j:P, 0:CHUNK])

        qv_bf = sbuf("qv_bf", [P, P, 4], BF16)
        nc.scalar.copy(qv_bf[:], qv_ps[:].rearrange("p t q -> p q t"))
        qv_codes = sbuf("qv_codes", [P, P], U32)
        qv_plane = draft_plane[:, 3 * T:3 * T + P]
        nc.vector.quantize_mx(out=qv_codes[:].bitcast(FP8X4), scales=qv_plane,
                              in_=qv_bf[:].rearrange("p q t -> p (q t)"))

        c0 = sbuf("c0", [P, T], F32)
        nc.scalar.copy(c0[:, 0:BANK], c0_ps[0][:])
        nc.scalar.copy(c0[:, BANK:T], c0_ps[1][:])

        b_ps = scores("b", qv_codes, qv_plane, BANK,
                      lambda j: draft_w[:, 2 * j * BANK:2 * (j + 1) * BANK].bitcast(FP4X4),
                      lambda j: draft_plane[:, j * BANK:(j + 1) * BANK])
        a_ps = scores("a", qv_codes, qv_plane, CHUNK,
                      lambda j: cache_w[:, j * CHUNK:(j + 1) * CHUNK].bitcast(FP8X4),
                      lambda j: packed[4 * j:P, CHUNK:2 * CHUNK])

        a = sbuf("a", [P, T], F32)
        b = sbuf("b", [P, T], F32)
        gb1 = sbuf("gb1", [P, HALF], F32)
        gc2 = sbuf("gc2", [P, HALF], F32)
        d1 = sbuf("d1", [P, HALF], F32)
        e1 = sbuf("e1", [P, HALF], F32)
        v2 = sbuf("v2", [P, HALF], F32)
        w = sbuf("w", [P, SLOTS], F32)
        r = sbuf("r", [P, SLOTS], F32)
        gc1_gb2 = sbuf("gc1_gb2", [P, 3 * 128], F32)
        gc1, gb2 = gc1_gb2[:, 128:384], gc1_gb2[:, 0:256]
        d2 = sbuf("d2", [P, HALF], F32)
        e2 = sbuf("e2", [P, HALF], F32)
        v1 = [d2[:, 0:128], e2[:, 0:128]]

        def look(window, lst, s):
            return window[:].indirect(lst[:, s.start // 16:s.stop // 16])

        def abs_v(dst, src):
            nc.vector.scalar_tensor_tensor(dst, src, -1.0, src, ALU.mult, ALU.max)

        h1, h2 = slice(0, HALF), slice(HALF, SLOTS)

        q1, q2, q3, q4 = [slice(128 * i, 128 * (i + 1)) for i in range(4)]
        nc.vector.tensor_copy(b[:, 0:BANK], b_ps[0][:])
        nc.scalar.copy(b[:, BANK:T], b_ps[1][:])
        nc.vector.tensor_copy(a[:, 0:BANK], a_ps[0][:])
        nc.vector.tensor_copy(a[:, BANK:T], a_ps[1][:])
        nc.scalar.activation(gb1[:], look(b, list_b, h1), ACT.Copy)
        nc.scalar.activation(gc1, look(c0, list_c, h1), ACT.Copy)
        nc.scalar.activation(gc2[:], look(c0, list_c, h2), ACT.Copy)
        nc.vector.tensor_tensor(d1[:], look(a, list_a, h1), gb1[:], ALU.subtract)
        for q in (q1, q2):
            nc.vector.tensor_tensor(e1[:, q], gc1[:, q], gb1[:, q], ALU.subtract)
        nc.vector.tensor_copy(gb2, look(b, list_b, h2))
        for q, v in zip((q1, q2), v1):
            nc.scalar.activation(w[:, q], d1[:, q], ACT.Abs)
            nc.scalar.activation(v, e1[:, q], ACT.Abs)
        for q, v in zip((q1, q2), v1):
            nc.vector.tensor_tensor(r[:, q], w[:, q], v, ALU.subtract)
        nc.scalar.activation(look(f1, list_r, h1), r[:, h1], ACT.Copy)
        nc.vector.tensor_tensor(d2[:], look(a, list_a, h2), gb2, ALU.subtract)
        nc.vector.tensor_tensor(e2[:], gc2[:], gb2, ALU.subtract)
        abs_v(w[:, h2], d2[:])
        abs_v(v2[:], e2[:])
        nc.vector.tensor_tensor(r[:, h2], w[:, h2], v2[:], ALU.subtract)
        nc.scalar.activation(look(f1, list_r, h2), r[:, h2], ACT.Copy)

        cc = sbuf("cc", [P, T], F32)
        nc.vector.tensor_tensor(cc[:, 0:BANK], c0_ps[0][:], f1[:, 0:BANK], ALU.add)
        nc.vector.tensor_tensor(cc[:, BANK:SPLIT], c0_ps[1][:, 0:SPLIT - BANK], f1[:, BANK:SPLIT], ALU.add)
        nc.gpsimd.tensor_tensor(cc[:, SPLIT:T], c0[:, SPLIT:T], f1[:, SPLIT:T], ALU.add)
        g2 = sbuf("g2", [P, HALF], F32)
        z = sbuf("z", [P, SLOTS], F32)
        y = sbuf("y", [P, SLOTS], F32)
        nc.vector.tensor_tensor(z[:, h1], look(cc, list_c, h1), w[:, h1], ALU.subtract)
        nc.scalar.activation(g2[:], look(cc, list_c, h2), ACT.Copy)
        nc.scalar.activation(y[:, h1], z[:, h1], ACT.Abs)
        for q, lo in ((q3, q1), (q4, q2)):
            nc.vector.tensor_tensor(z[:, q], g2[:, lo], w[:, q], ALU.subtract)
        nc.sync.dma_start(out[:, h1], y[:, h1])
        abs_v(y[:, q3], z[:, q3])
        nc.scalar.activation(y[:, q4], z[:, q4], ACT.Abs)
        nc.sync.dma_start(out[:, h2], y[:, h2])
